import numpy as np
import ml_dtypes


def mxq(x, axis, fmt="e4m3"):
    dtype, down = {"e4m3": (ml_dtypes.float8_e4m3fn, 7), "e5m2": (ml_dtypes.float8_e5m2, 14)}[fmt]
    v = np.moveaxis(np.asarray(x, np.float32).astype(ml_dtypes.bfloat16).astype(np.float64), axis, -1)
    blocks = v.reshape(v.shape[:-1] + (-1, 32))
    amax = np.abs(blocks).max(-1, keepdims=True)
    byte = np.maximum(np.where(amax > 0, np.frexp(amax)[1] - 1 + 127, 0) - down, 1)
    scale = np.exp2(byte - 127.0)
    codes = (blocks / scale).astype(np.float32).astype(dtype).astype(np.float64)
    return np.moveaxis((codes * scale).reshape(v.shape), -1, axis)


WIDE = False


def mx_kscale(k):
    if not WIDE:
        return np.ones(k)
    levels = np.array([10, -10, 5, -5, 0])
    if k % 512:
        return np.exp2(np.random.permutation(np.resize(levels, k // 32))).repeat(32)
    a = np.empty((k // 512, 16))
    for p in range(k // 512):
        a[p, :8] = np.random.permutation(np.resize(levels, 8))
        for g in range(8):
            far = levels[np.abs(levels - a[p, g]) >= 10]
            a[p, g + 8] = far[np.random.randint(len(far))]
    return np.exp2(a.ravel()).repeat(32)


def f64(x):
    return np.asarray(x).astype(np.float64)


def striped(idx):
    return np.tile(idx.reshape(-1, 16).T, (8, 1)).astype(np.uint16)


def unstriped(offs):
    return offs[:16].T.reshape(-1).astype(np.int64)


def pack_weight(w):
    k, n = w.shape
    w = f64(np.asarray(w, np.float32).astype(ml_dtypes.bfloat16)).reshape(k // 32, 32, n)
    amax = np.abs(w).max(1)
    byte = np.clip(np.where(amax > 0, np.frexp(amax)[1] - 1 + 127 - 7, 1), 1, 254)
    scaled = (w * np.exp2(127.0 - byte)[:, None, :]).reshape(k, n).astype(np.float32)
    words = np.ascontiguousarray(scaled.reshape(k // 512, 128, 4, n).transpose(0, 1, 3, 2)).astype(ml_dtypes.float8_e4m3fn).view(np.uint8)
    return words, np.ascontiguousarray(byte.astype(np.uint8).reshape(k // 512, 16, n))


def unpack_weight(words, scales):
    g, p, n, _ = words.shape
    vals = np.ascontiguousarray(words).view(ml_dtypes.float8_e4m3fn).astype(np.float64) * np.repeat(np.exp2(scales.astype(np.float64) - 127.0), 8, axis=1)[..., None]
    return vals.transpose(0, 1, 3, 2).reshape(g * 512, n)


K, T, S, V, N = 512, 4096, 1024, 512, 128


def setup_inputs():
    n = np.random.standard_normal
    s = mx_kscale(K)[:, None]
    packed_w1 = pack_weight(n((K, N)) / np.sqrt(K) / s)
    return {
        "xT": (n((K, T)) * s).astype(np.float32),
        "w1_words": packed_w1[0],
        "w1_scales": packed_w1[1],
        "offs": striped(np.random.permutation(T)[:S]),
        "win": striped(np.random.permutation(S)[:V]),
        "lose": striped(np.random.permutation(S)[:V]),
    }


def reference(xT, w1_words, w1_scales, offs, win, lose):
    xq = mxq(f64(xT)[:, unstriped(offs)], 0, "e4m3")
    y = unpack_weight(w1_words, w1_scales).T @ xq
    return np.tanh(y[:, unstriped(win)] - y[:, unstriped(lose)])

@@ -1,0 +1,109 @@
+from contextlib import ExitStack
+
+import concourse.mybir as mybir
+
+K, T, S, V, N = 512, 4096, 1024, 512, 128
+FLOPS = 2 * K * S * N
+
+F32 = mybir.dt.float32
+BF16 = mybir.dt.bfloat16
+I32 = mybir.dt.int32
+U32 = mybir.dt.uint32
+U16 = mybir.dt.uint16
+U8 = mybir.dt.uint8
+FP8X4 = mybir.dt.float8_e4m3fn_x4
+COPY = mybir.ActivationFunctionType.Copy
+TANH = mybir.ActivationFunctionType.Tanh
+
+P = 128
+PACK = 4
+HALF = S // 2
+PIECES = ((0, 256), (256, 512), (512, 768), (768, 896), (896, 1024))
+LAST_CHUNKS = ((0, 1024, "scalar"), (1024, 2048, "scalar"), (2048, 3072, "vector"), (3072, 3584, "scalar"), (3584, 4096, "scalar"))
+PAIR_PIECES = ((0, 384), (384, 512))
+
+
+def tile_picked_ranknet_tanh_e_kernel(tc, xT, w1_words, w1_scales, offs, win, lose, out):
+    nc = tc.nc
+    with ExitStack() as ctx:
+        keep = ctx.enter_context(tc.tile_pool(name="keep", bufs=1))
+        psum = ctx.enter_context(tc.psum_pool(name="psum", bufs=1))
+
+        offs_sb = keep.tile([P, S // 16], U16, name="offs_sb")
+        win_sb = keep.tile([P, V // 16], U16, name="win_sb")
+        lose_sb = keep.tile([P, V // 16], U16, name="lose_sb")
+        planes = [keep.tile([P, T], F32, name="plane%d" % t, align_bytes=64) for t in range(PACK)]
+        last_bf16 = keep.tile([P, T], BF16, name="last_bf16", align_bytes=64)
+        picked = [keep.tile([P, HALF, PACK], BF16, name="picked%d" % h, align_bytes=64) for h in range(2)]
+        w_codes = keep.tile([P, N], U32, name="w_codes", align_bytes=64)
+        w_scales = keep.tile([P, N], U8, name="w_scales", align_bytes=64)
+        warm_in = keep.tile([P, 8], F32, name="warm_in")
+        warm_out = keep.tile([P, 8], F32, name="warm_out")
+        y = keep.tile([P, S], F32, name="y", align_bytes=64)
+
+        nc.gpsimd.memset(warm_in[:], 0.0)
+        nc.gpsimd.memset(w_scales[:], 0)
+        nc.scalar.activation(warm_out[:], warm_in[:], TANH)
+
+        rows = xT.rearrange("(p t) w -> p t w", t=PACK)
+        nc.sync.dma_start(planes[0][:], rows[:, 0, :])
+        nc.sync.dma_start(offs_sb[:], offs)
+        for t in range(1, PACK - 1):
+            nc.sync.dma_start(planes[t][:], rows[:, t, :])
+        for a, b, who in LAST_CHUNKS:
+            nc.sync.dma_start(planes[PACK - 1][:, a:b], rows[:, PACK - 1, a:b])
+        nc.sync.dma_start(w_codes[:].bitcast(I32), w1_words[0].rearrange("p n t -> p (n t)").bitcast(I32))
+        for q in range(4):
+            nc.sync.dma_start(w_scales[32 * q : 32 * q + 4, :].bitcast(I32), w1_scales[0, 4 * q : 4 * q + 4, :].bitcast(I32))
+        nc.sync.dma_start(lose_sb[:], lose)
+        nc.sync.dma_start(win_sb[:], win)
+
+        def half_list(h):
+            return offs_sb[:, h * HALF // 16 : (h + 1) * HALF // 16]
+
+        for t in range(PACK - 1):
+            for h in range(2):
+                nc.vector.tensor_copy(picked[h][:, :, t], planes[t][:].indirect(half_list(h)))
+        for a, b, who in LAST_CHUNKS:
+            if who == "scalar":
+                nc.scalar.activation(last_bf16[:, a:b], planes[PACK - 1][:, a:b], COPY)
+            else:
+                nc.vector.tensor_copy(last_bf16[:, a:b], planes[PACK - 1][:, a:b])
+        nc.vector.tensor_copy(picked[0][:, :, PACK - 1], planes[PACK - 1][:].indirect(half_list(0)))
+        nc.scalar.activation(picked[1][:, :, PACK - 1], last_bf16[:].indirect(half_list(1)), COPY)
+
+        for i, (a, b) in enumerate(PIECES):
+            h, c = divmod(a, HALF)
+            codes = keep.tile([P, b - a], U32, name="codes%d" % i, align_bytes=64)
+            scales = keep.tile([P, b - a], U8, name="scales%d" % i, align_bytes=64)
+            nc.vector.quantize_mx(
+                out=codes[:].bitcast(FP8X4),
+                scales=scales[:],
+                in_=picked[h][:, c : c + b - a, :].rearrange("p w t -> p (w t)"),
+            )
+            acc = psum.tile([P, b - a], F32, name="acc%d" % i)
+            nc.tensor.matmul_mx(
+                out=acc[:],
+                lhsT=w_codes[:].bitcast(FP8X4),
+                lhsT_scale=w_scales[:],
+                rhs=codes[:].bitcast(FP8X4),
+                rhs_scale=scales[:],
+                start=True,
+                stop=True,
+            )
+            if i < len(PIECES) - 1:
+                nc.scalar.activation(y[:, a:b], acc[:], COPY)
+            else:
+                nc.vector.tensor_copy(y[:, a:b], acc[:])
+
+        losers = []
+        for a, b in PAIR_PIECES:
+            loser = keep.tile([P, b - a], F32, name="loser%d" % a)
+            nc.vector.tensor_copy(loser[:], y[:].indirect(lose_sb[:, a // 16 : b // 16]))
+            losers.append(loser)
+        for (a, b), loser in zip(PAIR_PIECES, losers):
+            diff = keep.tile([P, b - a], F32, name="diff%d" % a)
+            res = keep.tile([P, b - a], F32, name="res%d" % a)
+            nc.vector.tensor_tensor(diff[:], y[:].indirect(win_sb[:, a // 16 : b // 16]), loser[:], mybir.AluOpType.subtract)
+            nc.scalar.activation(res[:], diff[:], TANH)
+            (nc.scalar if b == V else nc.sync).dma_start(out[:, a:b], res[:])

@@ -19,7 +19,8 @@ P = 128
 PACK = 4
 HALF = S // 2
 PIECES = ((0, 256), (256, 512), (512, 768), (768, 896), (896, 1024))
-LAST_CHUNKS = ((0, 1024, "scalar"), (1024, 2048, "scalar"), (2048, 3072, "vector"), (3072, 3584, "scalar"), (3584, 4096, "scalar"))
+LAST_CHUNKS = ((0, 1024), (1024, 2048), (2048, 3072), (3072, 3584), (3584, 4096))
+CASTS = ((0, 1024, "scalar"), (1024, 2048, "scalar"), (2048, 3072, "scalar"), (3072, 3584, "vector"), (3584, 3840, "vector"), (3840, 4096, "scalar"))
 PAIR_PIECES = ((0, 384), (384, 512))
 
 
@@ -37,20 +38,16 @@ def tile_picked_ranknet_tanh_e_kernel(tc, xT, w1_words, w1_scales, offs, win, lo
         picked = [keep.tile([P, HALF, PACK], BF16, name="picked%d" % h, align_bytes=64) for h in range(2)]
         w_codes = keep.tile([P, N], U32, name="w_codes", align_bytes=64)
         w_scales = keep.tile([P, N], U8, name="w_scales", align_bytes=64)
-        warm_in = keep.tile([P, 8], F32, name="warm_in")
-        warm_out = keep.tile([P, 8], F32, name="warm_out")
         y = keep.tile([P, S], F32, name="y", align_bytes=64)
 
-        nc.gpsimd.memset(warm_in[:], 0.0)
         nc.gpsimd.memset(w_scales[:], 0)
-        nc.scalar.activation(warm_out[:], warm_in[:], TANH)
 
         rows = xT.rearrange("(p t) w -> p t w", t=PACK)
         nc.sync.dma_start(planes[0][:], rows[:, 0, :])
         nc.sync.dma_start(offs_sb[:], offs)
         for t in range(1, PACK - 1):
             nc.sync.dma_start(planes[t][:], rows[:, t, :])
-        for a, b, who in LAST_CHUNKS:
+        for a, b in LAST_CHUNKS:
             nc.sync.dma_start(planes[PACK - 1][:, a:b], rows[:, PACK - 1, a:b])
         nc.sync.dma_start(w_codes[:].bitcast(I32), w1_words[0].rearrange("p n t -> p (n t)").bitcast(I32))
         for q in range(4):
@@ -64,7 +61,7 @@ def tile_picked_ranknet_tanh_e_kernel(tc, xT, w1_words, w1_scales, offs, win, lo
         for t in range(PACK - 1):
             for h in range(2):
                 nc.vector.tensor_copy(picked[h][:, :, t], planes[t][:].indirect(half_list(h)))
-        for a, b, who in LAST_CHUNKS:
+        for a, b, who in CASTS:
             if who == "scalar":
                 nc.scalar.activation(last_bf16[:, a:b], planes[PACK - 1][:, a:b], COPY)
             else:

@@ -20,8 +20,8 @@ PACK = 4
 HALF = S // 2
 PIECES = ((0, 256), (256, 512), (512, 768), (768, 896), (896, 1024))
 LAST_CHUNKS = ((0, 1024), (1024, 2048), (2048, 3072), (3072, 3584), (3584, 4096))
-CASTS = ((0, 1024, "scalar"), (1024, 2048, "scalar"), (2048, 3072, "scalar"), (3072, 3584, "vector"), (3584, 3840, "vector"), (3840, 4096, "scalar"))
-PAIR_PIECES = ((0, 384), (384, 512))
+CASTS = ((0, 1024, "scalar"), (1024, 2048, "scalar"), (2048, 3072, "vector"), (3072, 3584, "scalar"), (3584, 4096, "scalar"))
+PAIR_PIECES = ((0, 192), (192, 384), (384, 512))
 
 
 def tile_picked_ranknet_tanh_e_kernel(tc, xT, w1_words, w1_scales, offs, win, lose, out):
@@ -88,19 +88,23 @@ def tile_picked_ranknet_tanh_e_kernel(tc, xT, w1_words, w1_scales, offs, win, lo
                 start=True,
                 stop=True,
             )
-            if i < len(PIECES) - 1:
+            if i != len(PIECES) - 2:
                 nc.scalar.activation(y[:, a:b], acc[:], COPY)
             else:
                 nc.vector.tensor_copy(y[:, a:b], acc[:])
 
-        losers = []
-        for a, b in PAIR_PIECES:
+        def fetch_losers(a, b):
             loser = keep.tile([P, b - a], F32, name="loser%d" % a)
             nc.vector.tensor_copy(loser[:], y[:].indirect(lose_sb[:, a // 16 : b // 16]))
-            losers.append(loser)
-        for (a, b), loser in zip(PAIR_PIECES, losers):
+            return loser
+
+        loser = fetch_losers(*PAIR_PIECES[0])
+        for i, (a, b) in enumerate(PAIR_PIECES):
+            last = i == len(PAIR_PIECES) - 1
+            ahead = None if last else fetch_losers(*PAIR_PIECES[i + 1])
             diff = keep.tile([P, b - a], F32, name="diff%d" % a)
             res = keep.tile([P, b - a], F32, name="res%d" % a)
             nc.vector.tensor_tensor(diff[:], y[:].indirect(win_sb[:, a // 16 : b // 16]), loser[:], mybir.AluOpType.subtract)
             nc.scalar.activation(res[:], diff[:], TANH)
-            (nc.scalar if b == V else nc.sync).dma_start(out[:, a:b], res[:])
+            (nc.scalar if last else nc.sync).dma_start(out[:, a:b], res[:])
+            loser = ahead

@@ -18,9 +18,9 @@ TANH = mybir.ActivationFunctionType.Tanh
 P = 128
 PACK = 4
 HALF = S // 2
-PIECES = ((0, 256), (256, 512), (512, 768), (768, 896), (896, 1024))
-LAST_CHUNKS = ((0, 1024), (1024, 2048), (2048, 3072), (3072, 3584), (3584, 4096))
-CASTS = ((0, 1024, "scalar"), (1024, 2048, "scalar"), (2048, 3072, "vector"), (3072, 3584, "scalar"), (3584, 4096, "scalar"))
+PIECES = tuple((a, a + 128) for a in range(0, S, 128))
+LAST_CHUNKS = ((0, 2048), (2048, 3584), (3584, 4096))
+CASTS = ((0, 1280, "scalar"), (1280, 2048, "vector"), (2048, 3072, "vector"), (3072, 3584, "scalar"), (3584, 3968, "scalar"), (3968, 4096, "vector"))
 PAIR_PIECES = ((0, 192), (192, 384), (384, 512))
 
 
@@ -69,6 +69,7 @@ def tile_picked_ranknet_tanh_e_kernel(tc, xT, w1_words, w1_scales, offs, win, lo
         nc.vector.tensor_copy(picked[0][:, :, PACK - 1], planes[PACK - 1][:].indirect(half_list(0)))
         nc.scalar.activation(picked[1][:, :, PACK - 1], last_bf16[:].indirect(half_list(1)), COPY)
 
+        accs = []
         for i, (a, b) in enumerate(PIECES):
             h, c = divmod(a, HALF)
             codes = keep.tile([P, b - a], U32, name="codes%d" % i, align_bytes=64)
@@ -88,10 +89,12 @@ def tile_picked_ranknet_tanh_e_kernel(tc, xT, w1_words, w1_scales, offs, win, lo
                 start=True,
                 stop=True,
             )
-            if i != len(PIECES) - 2:
-                nc.scalar.activation(y[:, a:b], acc[:], COPY)
+            accs.append(acc)
+        for i, (a, b) in enumerate(PIECES):
+            if i in (4, 6):
+                nc.vector.tensor_copy(y[:, a:b], accs[i][:])
             else:
-                nc.vector.tensor_copy(y[:, a:b], acc[:])
+                nc.scalar.activation(y[:, a:b], accs[i][:], COPY)
 
         def fetch_losers(a, b):
             loser = keep.tile([P, b - a], F32, name="loser%d" % a)

@@ -19,9 +19,11 @@ P = 128
 PACK = 4
 HALF = S // 2
 PIECES = tuple((a, a + 128) for a in range(0, S, 128))
-LAST_CHUNKS = ((0, 2048), (2048, 3584), (3584, 4096))
-CASTS = ((0, 1280, "scalar"), (1280, 2048, "vector"), (2048, 3072, "vector"), (3072, 3584, "scalar"), (3584, 3968, "scalar"), (3968, 4096, "vector"))
-PAIR_PIECES = ((0, 192), (192, 384), (384, 512))
+LAST_CHUNKS = ((0, 2496), (2496, 3712), (3712, 4096))
+CASTS = ((0, 1280, "scalar"), (1280, 2496, "vector"), (2496, 3424, "vector"), (3424, 3712, "scalar"), (3712, 4096, "scalar"))
+LOSER_PIECES = ((0, 256), (256, 512))
+PAIR_PIECES = ((0, 256), (256, 384), (384, 448), (448, 512))
+STORES = ((0, 256), (256, 384), (384, 512))
 
 
 def tile_picked_ranknet_tanh_e_kernel(tc, xT, w1_words, w1_scales, offs, win, lose, out):
@@ -96,18 +98,13 @@ def tile_picked_ranknet_tanh_e_kernel(tc, xT, w1_words, w1_scales, offs, win, lo
             else:
                 nc.scalar.activation(y[:, a:b], accs[i][:], COPY)
 
-        def fetch_losers(a, b):
-            loser = keep.tile([P, b - a], F32, name="loser%d" % a)
-            nc.vector.tensor_copy(loser[:], y[:].indirect(lose_sb[:, a // 16 : b // 16]))
-            return loser
-
-        loser = fetch_losers(*PAIR_PIECES[0])
-        for i, (a, b) in enumerate(PAIR_PIECES):
-            last = i == len(PAIR_PIECES) - 1
-            ahead = None if last else fetch_losers(*PAIR_PIECES[i + 1])
-            diff = keep.tile([P, b - a], F32, name="diff%d" % a)
-            res = keep.tile([P, b - a], F32, name="res%d" % a)
-            nc.vector.tensor_tensor(diff[:], y[:].indirect(win_sb[:, a // 16 : b // 16]), loser[:], mybir.AluOpType.subtract)
-            nc.scalar.activation(res[:], diff[:], TANH)
-            (nc.scalar if last else nc.sync).dma_start(out[:, a:b], res[:])
-            loser = ahead
+        loser = keep.tile([P, V], F32, name="loser")
+        diff = keep.tile([P, V], F32, name="diff")
+        res = keep.tile([P, V], F32, name="res")
+        for a, b in LOSER_PIECES:
+            nc.vector.tensor_copy(loser[:, a:b], y[:].indirect(lose_sb[:, a // 16 : b // 16]))
+        for a, b in PAIR_PIECES:
+            nc.vector.tensor_tensor(diff[:, a:b], y[:].indirect(win_sb[:, a // 16 : b // 16]), loser[:, a:b], mybir.AluOpType.subtract)
+            nc.scalar.activation(res[:, a:b], diff[:, a:b], TANH)
+        for a, b in STORES:
+            (nc.scalar if b == V else nc.sync).dma_start(out[:, a:b], res[:, a:b])

@@ -20,7 +20,8 @@ PACK = 4
 HALF = S // 2
 PIECES = tuple((a, a + 128) for a in range(0, S, 128))
 LAST_CHUNKS = ((0, 2496), (2496, 3712), (3712, 4096))
-CASTS = ((0, 1280, "scalar"), (1280, 2496, "vector"), (2496, 3424, "vector"), (3424, 3712, "scalar"), (3712, 4096, "scalar"))
+CASTS = ((0, 960, "scalar"), (960, 2496, "vector"), (2496, 3392, "vector"), (3392, 3712, "scalar"), (3712, 4096, "scalar"))
+EARLY = (2, 0, 1)
 LOSER_PIECES = ((0, 256), (256, 512))
 PAIR_PIECES = ((0, 256), (256, 384), (384, 448), (448, 512))
 STORES = ((0, 256), (256, 384), (384, 512))
@@ -38,6 +39,7 @@ def tile_picked_ranknet_tanh_e_kernel(tc, xT, w1_words, w1_scales, offs, win, lo
         planes = [keep.tile([P, T], F32, name="plane%d" % t, align_bytes=64) for t in range(PACK)]
         last_bf16 = keep.tile([P, T], BF16, name="last_bf16", align_bytes=64)
         picked = [keep.tile([P, HALF, PACK], BF16, name="picked%d" % h, align_bytes=64) for h in range(2)]
+        pairs = keep.tile([P, HALF, 2], BF16, name="pairs", align_bytes=64)
         w_codes = keep.tile([P, N], U32, name="w_codes", align_bytes=64)
         w_scales = keep.tile([P, N], U8, name="w_scales", align_bytes=64)
         y = keep.tile([P, S], F32, name="y", align_bytes=64)
@@ -45,9 +47,9 @@ def tile_picked_ranknet_tanh_e_kernel(tc, xT, w1_words, w1_scales, offs, win, lo
         nc.gpsimd.memset(w_scales[:], 0)
 
         rows = xT.rearrange("(p t) w -> p t w", t=PACK)
-        nc.sync.dma_start(planes[0][:], rows[:, 0, :])
+        nc.sync.dma_start(planes[EARLY[0]][:], rows[:, EARLY[0], :])
         nc.sync.dma_start(offs_sb[:], offs)
-        for t in range(1, PACK - 1):
+        for t in EARLY[1:]:
             nc.sync.dma_start(planes[t][:], rows[:, t, :])
         for a, b in LAST_CHUNKS:
             nc.sync.dma_start(planes[PACK - 1][:, a:b], rows[:, PACK - 1, a:b])
@@ -60,9 +62,11 @@ def tile_picked_ranknet_tanh_e_kernel(tc, xT, w1_words, w1_scales, offs, win, lo
         def half_list(h):
             return offs_sb[:, h * HALF // 16 : (h + 1) * HALF // 16]
 
-        for t in range(PACK - 1):
-            for h in range(2):
-                nc.vector.tensor_copy(picked[h][:, :, t], planes[t][:].indirect(half_list(h)))
+        for t in EARLY:
+            first_half = pairs[:, :, t] if t < 2 else picked[0][:, :, t]
+            nc.vector.tensor_copy(first_half, planes[t][:].indirect(half_list(0)))
+            nc.vector.tensor_copy(picked[1][:, :, t], planes[t][:].indirect(half_list(1)))
+        nc.scalar.activation(picked[0][:, :, 0:2], pairs[:], COPY)
         for a, b, who in CASTS:
             if who == "scalar":
                 nc.scalar.activation(last_bf16[:, a:b], planes[PACK - 1][:, a:b], COPY)

@@ -20,7 +20,7 @@ PACK = 4
 HALF = S // 2
 PIECES = tuple((a, a + 128) for a in range(0, S, 128))
 LAST_CHUNKS = ((0, 2496), (2496, 3712), (3712, 4096))
-CASTS = ((0, 960, "scalar"), (960, 2496, "vector"), (2496, 3392, "vector"), (3392, 3712, "scalar"), (3712, 4096, "scalar"))
+CASTS = ((0, 960, "scalar"), (960, 2496, "vector"), (2496, 3360, "vector"), (3360, 3712, "scalar"), (3712, 4096, "scalar"))
 EARLY = (2, 0, 1)
 LOSER_PIECES = ((0, 256), (256, 512))
 PAIR_PIECES = ((0, 256), (256, 384), (384, 448), (448, 512))
@@ -39,7 +39,7 @@ def tile_picked_ranknet_tanh_e_kernel(tc, xT, w1_words, w1_scales, offs, win, lo
         planes = [keep.tile([P, T], F32, name="plane%d" % t, align_bytes=64) for t in range(PACK)]
         last_bf16 = keep.tile([P, T], BF16, name="last_bf16", align_bytes=64)
         picked = [keep.tile([P, HALF, PACK], BF16, name="picked%d" % h, align_bytes=64) for h in range(2)]
-        pairs = keep.tile([P, HALF, 2], BF16, name="pairs", align_bytes=64)
+        dense = [keep.tile([P, HALF], BF16, name="dense%d" % i, align_bytes=64) for i in range(PACK)]
         w_codes = keep.tile([P, N], U32, name="w_codes", align_bytes=64)
         w_scales = keep.tile([P, N], U8, name="w_scales", align_bytes=64)
         y = keep.tile([P, S], F32, name="y", align_bytes=64)
@@ -63,10 +63,17 @@ def tile_picked_ranknet_tanh_e_kernel(tc, xT, w1_words, w1_scales, offs, win, lo
             return offs_sb[:, h * HALF // 16 : (h + 1) * HALF // 16]
 
         for t in EARLY:
-            first_half = pairs[:, :, t] if t < 2 else picked[0][:, :, t]
-            nc.vector.tensor_copy(first_half, planes[t][:].indirect(half_list(0)))
-            nc.vector.tensor_copy(picked[1][:, :, t], planes[t][:].indirect(half_list(1)))
-        nc.scalar.activation(picked[0][:, :, 0:2], pairs[:], COPY)
+            nc.vector.tensor_copy(dense[t][:], planes[t][:].indirect(half_list(1)))
+            nc.scalar.activation(picked[1][:, :, t], dense[t][:], COPY)
+            if t == EARLY[-1]:
+                for a in (0, HALF // 2):
+                    b = a + HALF // 2
+                    nc.vector.tensor_copy(dense[PACK - 1][:, a:b], planes[t][:].indirect(offs_sb[:, a // 16 : b // 16]))
+                for a in (0, HALF // 2):
+                    b = a + HALF // 2
+                    nc.vector.tensor_copy(picked[0][:, a:b, t], dense[PACK - 1][:, a:b])
+            else:
+                nc.vector.tensor_copy(picked[0][:, :, t], planes[t][:].indirect(half_list(0)))
         for a, b, who in CASTS:
             if who == "scalar":
                 nc.scalar.activation(last_bf16[:, a:b], planes[PACK - 1][:, a:b], COPY)

@@ -18,10 +18,12 @@ TANH = mybir.ActivationFunctionType.Tanh
 P = 128
 PACK = 4
 HALF = S // 2
-PIECES = tuple((a, a + 128) for a in range(0, S, 128))
+PIECES = tuple((a, a + 128) for a in range(0, S - 128, 128)) + ((S - 128, S - 64), (S - 64, S))
+BANKS = 8
+VECTOR_BANKS = (4, 6)
 LAST_CHUNKS = ((0, 2496), (2496, 3712), (3712, 4096))
-CASTS = ((0, 960, "scalar"), (960, 2496, "vector"), (2496, 3360, "vector"), (3360, 3712, "scalar"), (3712, 4096, "scalar"))
-EARLY = (2, 0, 1)
+CASTS = ((0, 960, "scalar"), (960, 2496, "vector"), (2496, 3392, "vector"), (3392, 3712, "scalar"), (3712, 4096, "scalar"))
+EARLY = (0, 1, 2)
 LOSER_PIECES = ((0, 256), (256, 512))
 PAIR_PIECES = ((0, 256), (256, 384), (384, 448), (448, 512))
 STORES = ((0, 256), (256, 384), (384, 512))
@@ -39,7 +41,7 @@ def tile_picked_ranknet_tanh_e_kernel(tc, xT, w1_words, w1_scales, offs, win, lo
         planes = [keep.tile([P, T], F32, name="plane%d" % t, align_bytes=64) for t in range(PACK)]
         last_bf16 = keep.tile([P, T], BF16, name="last_bf16", align_bytes=64)
         picked = [keep.tile([P, HALF, PACK], BF16, name="picked%d" % h, align_bytes=64) for h in range(2)]
-        dense = [keep.tile([P, HALF], BF16, name="dense%d" % i, align_bytes=64) for i in range(PACK)]
+        dense = [keep.tile([P, HALF], BF16, name="dense%d" % i, align_bytes=64) for i in range(PACK - 1)]
         w_codes = keep.tile([P, N], U32, name="w_codes", align_bytes=64)
         w_scales = keep.tile([P, N], U8, name="w_scales", align_bytes=64)
         y = keep.tile([P, S], F32, name="y", align_bytes=64)
@@ -47,9 +49,8 @@ def tile_picked_ranknet_tanh_e_kernel(tc, xT, w1_words, w1_scales, offs, win, lo
         nc.gpsimd.memset(w_scales[:], 0)
 
         rows = xT.rearrange("(p t) w -> p t w", t=PACK)
-        nc.sync.dma_start(planes[EARLY[0]][:], rows[:, EARLY[0], :])
         nc.sync.dma_start(offs_sb[:], offs)
-        for t in EARLY[1:]:
+        for t in EARLY:
             nc.sync.dma_start(planes[t][:], rows[:, t, :])
         for a, b in LAST_CHUNKS:
             nc.sync.dma_start(planes[PACK - 1][:, a:b], rows[:, PACK - 1, a:b])
@@ -65,15 +66,7 @@ def tile_picked_ranknet_tanh_e_kernel(tc, xT, w1_words, w1_scales, offs, win, lo
         for t in EARLY:
             nc.vector.tensor_copy(dense[t][:], planes[t][:].indirect(half_list(1)))
             nc.scalar.activation(picked[1][:, :, t], dense[t][:], COPY)
-            if t == EARLY[-1]:
-                for a in (0, HALF // 2):
-                    b = a + HALF // 2
-                    nc.vector.tensor_copy(dense[PACK - 1][:, a:b], planes[t][:].indirect(offs_sb[:, a // 16 : b // 16]))
-                for a in (0, HALF // 2):
-                    b = a + HALF // 2
-                    nc.vector.tensor_copy(picked[0][:, a:b, t], dense[PACK - 1][:, a:b])
-            else:
-                nc.vector.tensor_copy(picked[0][:, :, t], planes[t][:].indirect(half_list(0)))
+            nc.vector.tensor_copy(picked[0][:, :, t], planes[t][:].indirect(half_list(0)))
         for a, b, who in CASTS:
             if who == "scalar":
                 nc.scalar.activation(last_bf16[:, a:b], planes[PACK - 1][:, a:b], COPY)
@@ -82,7 +75,7 @@ def tile_picked_ranknet_tanh_e_kernel(tc, xT, w1_words, w1_scales, offs, win, lo
         nc.vector.tensor_copy(picked[0][:, :, PACK - 1], planes[PACK - 1][:].indirect(half_list(0)))
         nc.scalar.activation(picked[1][:, :, PACK - 1], last_bf16[:].indirect(half_list(1)), COPY)
 
-        accs = []
+        for_vector = []
         for i, (a, b) in enumerate(PIECES):
             h, c = divmod(a, HALF)
             codes = keep.tile([P, b - a], U32, name="codes%d" % i, align_bytes=64)
@@ -92,7 +85,7 @@ def tile_picked_ranknet_tanh_e_kernel(tc, xT, w1_words, w1_scales, offs, win, lo
                 scales=scales[:],
                 in_=picked[h][:, c : c + b - a, :].rearrange("p w t -> p (w t)"),
             )
-            acc = psum.tile([P, b - a], F32, name="acc%d" % i)
+            acc = psum.tile([P, b - a], F32, name="acc%d" % (i % BANKS))
             nc.tensor.matmul_mx(
                 out=acc[:],
                 lhsT=w_codes[:].bitcast(FP8X4),
@@ -102,12 +95,12 @@ def tile_picked_ranknet_tanh_e_kernel(tc, xT, w1_words, w1_scales, offs, win, lo
                 start=True,
                 stop=True,
             )
-            accs.append(acc)
-        for i, (a, b) in enumerate(PIECES):
-            if i in (4, 6):
-                nc.vector.tensor_copy(y[:, a:b], accs[i][:])
+            if i in VECTOR_BANKS:
+                for_vector.append((a, b, acc))
             else:
-                nc.scalar.activation(y[:, a:b], accs[i][:], COPY)
+                nc.scalar.activation(y[:, a:b], acc[:], COPY)
+        for a, b, acc in for_vector:
+            nc.vector.tensor_copy(y[:, a:b], acc[:])
 
         loser = keep.tile([P, V], F32, name="loser")
         diff = keep.tile([P, V], F32, name="diff")

@@ -21,8 +21,8 @@ HALF = S // 2
 PIECES = tuple((a, a + 128) for a in range(0, S - 128, 128)) + ((S - 128, S - 64), (S - 64, S))
 BANKS = 8
 VECTOR_BANKS = (4, 6)
-LAST_CHUNKS = ((0, 2496), (2496, 3712), (3712, 4096))
-CASTS = ((0, 960, "scalar"), (960, 2496, "vector"), (2496, 3392, "vector"), (3392, 3712, "scalar"), (3712, 4096, "scalar"))
+LAST_CHUNKS = ((0, 2880), (2880, 3840), (3840, 4096))
+CASTS = ((0, 960, "scalar"), (960, 2880, "vector"), (2880, 3520, "vector"), (3520, 3840, "scalar"), (3840, 4096, "scalar"))
 EARLY = (0, 1, 2)
 LOSER_PIECES = ((0, 256), (256, 512))
 PAIR_PIECES = ((0, 256), (256, 384), (384, 448), (448, 512))
@@ -46,11 +46,12 @@ def tile_picked_ranknet_tanh_e_kernel(tc, xT, w1_words, w1_scales, offs, win, lo
         w_scales = keep.tile([P, N], U8, name="w_scales", align_bytes=64)
         y = keep.tile([P, S], F32, name="y", align_bytes=64)
 
-        nc.gpsimd.memset(w_scales[:], 0)
+        nc.vector.memset(w_scales[:].bitcast(I32), 0)
 
         rows = xT.rearrange("(p t) w -> p t w", t=PACK)
+        nc.sync.dma_start(planes[EARLY[0]][:], rows[:, EARLY[0], :])
         nc.sync.dma_start(offs_sb[:], offs)
-        for t in EARLY:
+        for t in EARLY[1:]:
             nc.sync.dma_start(planes[t][:], rows[:, t, :])
         for a, b in LAST_CHUNKS:
             nc.sync.dma_start(planes[PACK - 1][:, a:b], rows[:, PACK - 1, a:b])

@@ -18,9 +18,10 @@ TANH = mybir.ActivationFunctionType.Tanh
 P = 128
 PACK = 4
 HALF = S // 2
-PIECES = tuple((a, a + 128) for a in range(0, S - 128, 128)) + ((S - 128, S - 64), (S - 64, S))
+WIDTHS = (128, 128, 128, 128, 64, 128, 128, 128, 64)
+PIECES = tuple((sum(WIDTHS[:i]), sum(WIDTHS[: i + 1])) for i in range(len(WIDTHS)))
 BANKS = 8
-VECTOR_BANKS = (4, 6)
+VECTOR_BANKS = (5, 7)
 LAST_CHUNKS = ((0, 2880), (2880, 3840), (3840, 4096))
 CASTS = ((0, 960, "scalar"), (960, 2880, "vector"), (2880, 3520, "vector"), (3520, 3840, "scalar"), (3840, 4096, "scalar"))
 EARLY = (0, 1, 2)
@@ -66,11 +67,11 @@ def tile_picked_ranknet_tanh_e_kernel(tc, xT, w1_words, w1_scales, offs, win, lo
 
         for t in EARLY:
             nc.vector.tensor_copy(dense[t][:], planes[t][:].indirect(half_list(1)))
-            nc.scalar.activation(picked[1][:, :, t], dense[t][:], COPY)
+            nc.scalar.copy(picked[1][:, :, t], dense[t][:])
             nc.vector.tensor_copy(picked[0][:, :, t], planes[t][:].indirect(half_list(0)))
         for a, b, who in CASTS:
             if who == "scalar":
-                nc.scalar.activation(last_bf16[:, a:b], planes[PACK - 1][:, a:b], COPY)
+                nc.scalar.copy(last_bf16[:, a:b], planes[PACK - 1][:, a:b])
             else:
                 nc.vector.tensor_copy(last_bf16[:, a:b], planes[PACK - 1][:, a:b])
         nc.vector.tensor_copy(picked[0][:, :, PACK - 1], planes[PACK - 1][:].indirect(half_list(0)))
@@ -99,7 +100,7 @@ def tile_picked_ranknet_tanh_e_kernel(tc, xT, w1_words, w1_scales, offs, win, lo
             if i in VECTOR_BANKS:
                 for_vector.append((a, b, acc))
             else:
-                nc.scalar.activation(y[:, a:b], acc[:], COPY)
+                nc.scalar.copy(y[:, a:b], acc[:])
         for a, b, acc in for_vector:
             nc.vector.tensor_copy(y[:, a:b], acc[:])
 

@@ -23,7 +23,7 @@ PIECES = tuple((sum(WIDTHS[:i]), sum(WIDTHS[: i + 1])) for i in range(len(WIDTHS
 BANKS = 8
 VECTOR_BANKS = (5, 7)
 LAST_CHUNKS = ((0, 2880), (2880, 3840), (3840, 4096))
-CASTS = ((0, 960, "scalar"), (960, 2880, "vector"), (2880, 3520, "vector"), (3520, 3840, "scalar"), (3840, 4096, "scalar"))
+CASTS = ((0, 960, "scalar"), (960, 2880, "vector"), (2880, 3520, "vector"), (3520, 3840, "scalar"), (3840, 4032, "scalar"), (4032, 4096, "vector"))
 EARLY = (0, 1, 2)
 LOSER_PIECES = ((0, 256), (256, 512))
 PAIR_PIECES = ((0, 256), (256, 384), (384, 448), (448, 512))

@@ -23,7 +23,7 @@ PIECES = tuple((sum(WIDTHS[:i]), sum(WIDTHS[: i + 1])) for i in range(len(WIDTHS
 BANKS = 8
 VECTOR_BANKS = (5, 7)
 LAST_CHUNKS = ((0, 2880), (2880, 3840), (3840, 4096))
-CASTS = ((0, 960, "scalar"), (960, 2880, "vector"), (2880, 3520, "vector"), (3520, 3840, "scalar"), (3840, 4032, "scalar"), (4032, 4096, "vector"))
+CASTS = ((0, 1024, "scalar"), (1024, 2880, "vector"), (2880, 3488, "vector"), (3488, 3840, "scalar"), (3840, 4096, "scalar"))
 EARLY = (0, 1, 2)
 LOSER_PIECES = ((0, 256), (256, 512))
 PAIR_PIECES = ((0, 256), (256, 384), (384, 448), (448, 512))
@@ -66,8 +66,10 @@ def tile_picked_ranknet_tanh_e_kernel(tc, xT, w1_words, w1_scales, offs, win, lo
             return offs_sb[:, h * HALF // 16 : (h + 1) * HALF // 16]
 
         for t in EARLY:
-            nc.vector.tensor_copy(dense[t][:], planes[t][:].indirect(half_list(1)))
-            nc.scalar.copy(picked[1][:, :, t], dense[t][:])
+            cut = HALF // 2 if t == EARLY[-1] else HALF
+            for a in range(0, HALF, cut):
+                nc.vector.tensor_copy(dense[t][:, a : a + cut], planes[t][:].indirect(offs_sb[:, (HALF + a) // 16 : (HALF + a + cut) // 16]))
+                nc.scalar.copy(picked[1][:, a : a + cut, t], dense[t][:, a : a + cut])
             nc.vector.tensor_copy(picked[0][:, :, t], planes[t][:].indirect(half_list(0)))
         for a, b, who in CASTS:
             if who == "scalar":

@@ -23,7 +23,7 @@ PIECES = tuple((sum(WIDTHS[:i]), sum(WIDTHS[: i + 1])) for i in range(len(WIDTHS
 BANKS = 8
 VECTOR_BANKS = (5, 7)
 LAST_CHUNKS = ((0, 2880), (2880, 3840), (3840, 4096))
-CASTS = ((0, 1024, "scalar"), (1024, 2880, "vector"), (2880, 3488, "vector"), (3488, 3840, "scalar"), (3840, 4096, "scalar"))
+CASTS = ((0, 1024, "scalar"), (1024, 2880, "vector"), (2880, 3488, "vector"), (3488, 3840, "scalar"), (3840, 4032, "scalar"), (4032, 4096, "vector"))
 EARLY = (0, 1, 2)
 LOSER_PIECES = ((0, 256), (256, 512))
 PAIR_PIECES = ((0, 256), (256, 384), (384, 448), (448, 512))

@@ -23,7 +23,7 @@ PIECES = tuple((sum(WIDTHS[:i]), sum(WIDTHS[: i + 1])) for i in range(len(WIDTHS
 BANKS = 8
 VECTOR_BANKS = (5, 7)
 LAST_CHUNKS = ((0, 2880), (2880, 3840), (3840, 4096))
-CASTS = ((0, 1024, "scalar"), (1024, 2880, "vector"), (2880, 3488, "vector"), (3488, 3840, "scalar"), (3840, 4032, "scalar"), (4032, 4096, "vector"))
+CASTS = ((0, 1024, "scalar"), (1024, 2880, "vector"), (2880, 3488, "vector"), (3488, 3840, "scalar"), (3840, 4064, "scalar"), (4064, 4096, "vector"))
 EARLY = (0, 1, 2)
 LOSER_PIECES = ((0, 256), (256, 512))
 PAIR_PIECES = ((0, 256), (256, 384), (384, 448), (448, 512))

@@ -24,7 +24,7 @@ BANKS = 8
 VECTOR_BANKS = (5, 7)
 LAST_CHUNKS = ((0, 2880), (2880, 3840), (3840, 4096))
 CASTS = ((0, 1024, "scalar"), (1024, 2880, "vector"), (2880, 3488, "vector"), (3488, 3840, "scalar"), (3840, 4064, "scalar"), (4064, 4096, "vector"))
-EARLY = (0, 1, 2)
+EARLY = (2, 0, 1)
 LOSER_PIECES = ((0, 256), (256, 512))
 PAIR_PIECES = ((0, 256), (256, 384), (384, 448), (448, 512))
 STORES = ((0, 256), (256, 384), (384, 512))
@@ -66,10 +66,11 @@ def tile_picked_ranknet_tanh_e_kernel(tc, xT, w1_words, w1_scales, offs, win, lo
             return offs_sb[:, h * HALF // 16 : (h + 1) * HALF // 16]
 
         for t in EARLY:
-            cut = HALF // 2 if t == EARLY[-1] else HALF
-            for a in range(0, HALF, cut):
-                nc.vector.tensor_copy(dense[t][:, a : a + cut], planes[t][:].indirect(offs_sb[:, (HALF + a) // 16 : (HALF + a + cut) // 16]))
-                nc.scalar.copy(picked[1][:, a : a + cut, t], dense[t][:, a : a + cut])
+            nc.vector.tensor_copy(dense[t][:], planes[t][:].indirect(half_list(1)))
+            shared = HALF if t == EARLY[0] else HALF // 2
+            nc.scalar.copy(picked[1][:, :shared, t], dense[t][:, :shared])
+            if shared < HALF:
+                nc.gpsimd.tensor_copy(picked[1][:, shared:, t], dense[t][:, shared:])
             nc.vector.tensor_copy(picked[0][:, :, t], planes[t][:].indirect(half_list(0)))
         for a, b, who in CASTS:
             if who == "scalar":

@@ -14,20 +14,21 @@ U8 = mybir.dt.uint8
 FP8X4 = mybir.dt.float8_e4m3fn_x4
 COPY = mybir.ActivationFunctionType.Copy
 TANH = mybir.ActivationFunctionType.Tanh
+SUBTRACT = mybir.AluOpType.subtract
 
 P = 128
 PACK = 4
 HALF = S // 2
-WIDTHS = (128, 128, 128, 128, 64, 128, 128, 128, 64)
-PIECES = tuple((sum(WIDTHS[:i]), sum(WIDTHS[: i + 1])) for i in range(len(WIDTHS)))
+BY_GPSIMD = 256
+LAST_GATHERS = ((0, 128), (128, 256), (256, 512))
+LAST_PLACINGS = ((0, 128, "gpsimd"), (128, 256, "gpsimd"), (256, 384, "scalar"), (384, 512, "scalar"))
+PIECES = ((512, 640), (0, 128), (128, 256), (256, 384), (384, 512), (640, 768), (768, 896), (896, 960), (960, 1024))
 BANKS = 8
-VECTOR_BANKS = (5, 7)
-LAST_CHUNKS = ((0, 2880), (2880, 3840), (3840, 4096))
-CASTS = ((0, 1024, "scalar"), (1024, 2880, "vector"), (2880, 3488, "vector"), (3488, 3840, "scalar"), (3840, 4064, "scalar"), (4064, 4096, "vector"))
-EARLY = (2, 0, 1)
-LOSER_PIECES = ((0, 256), (256, 512))
-PAIR_PIECES = ((0, 256), (256, 384), (384, 448), (448, 512))
-STORES = ((0, 256), (256, 384), (384, 512))
+VECTOR_PIECES = (5, 7)
+LOSERS = ((0, 96, "vector"), (96, 192, "vector"), (192, 320, "scalar"), (320, 448, "scalar"), (448, 512, "scalar"))
+PAIR_PIECES = ((0, 96), (96, 192), (192, 320), (320, 448), (448, 512))
+TANH_PIECES = ((0, 192), (192, 320), (320, 448), (448, 512))
+STORES = ((0, 320), (320, 448), (448, 512))
 
 
 def tile_picked_ranknet_tanh_e_kernel(tc, xT, w1_words, w1_scales, offs, win, lose, out):
@@ -40,9 +41,8 @@ def tile_picked_ranknet_tanh_e_kernel(tc, xT, w1_words, w1_scales, offs, win, lo
         win_sb = keep.tile([P, V // 16], U16, name="win_sb")
         lose_sb = keep.tile([P, V // 16], U16, name="lose_sb")
         planes = [keep.tile([P, T], F32, name="plane%d" % t, align_bytes=64) for t in range(PACK)]
-        last_bf16 = keep.tile([P, T], BF16, name="last_bf16", align_bytes=64)
         picked = [keep.tile([P, HALF, PACK], BF16, name="picked%d" % h, align_bytes=64) for h in range(2)]
-        dense = [keep.tile([P, HALF], BF16, name="dense%d" % i, align_bytes=64) for i in range(PACK - 1)]
+        dense = [keep.tile([P, HALF], BF16, name="dense%d" % t, align_bytes=64) for t in range(PACK - 1)]
         w_codes = keep.tile([P, N], U32, name="w_codes", align_bytes=64)
         w_scales = keep.tile([P, N], U8, name="w_scales", align_bytes=64)
         y = keep.tile([P, S], F32, name="y", align_bytes=64)
@@ -50,43 +50,50 @@ def tile_picked_ranknet_tanh_e_kernel(tc, xT, w1_words, w1_scales, offs, win, lo
         nc.vector.memset(w_scales[:].bitcast(I32), 0)
 
         rows = xT.rearrange("(p t) w -> p t w", t=PACK)
-        nc.sync.dma_start(planes[EARLY[0]][:], rows[:, EARLY[0], :])
+        nc.sync.dma_start(planes[0][:], rows[:, 0, :])
         nc.sync.dma_start(offs_sb[:], offs)
-        for t in EARLY[1:]:
+        for t in range(1, PACK):
             nc.sync.dma_start(planes[t][:], rows[:, t, :])
-        for a, b in LAST_CHUNKS:
-            nc.sync.dma_start(planes[PACK - 1][:, a:b], rows[:, PACK - 1, a:b])
         nc.sync.dma_start(w_codes[:].bitcast(I32), w1_words[0].rearrange("p n t -> p (n t)").bitcast(I32))
         for q in range(4):
             nc.sync.dma_start(w_scales[32 * q : 32 * q + 4, :].bitcast(I32), w1_scales[0, 4 * q : 4 * q + 4, :].bitcast(I32))
         nc.sync.dma_start(lose_sb[:], lose)
         nc.sync.dma_start(win_sb[:], win)
 
-        def half_list(h):
-            return offs_sb[:, h * HALF // 16 : (h + 1) * HALF // 16]
+        def entries(a, b):
+            return offs_sb[:, a // 16 : b // 16]
 
-        for t in EARLY:
-            nc.vector.tensor_copy(dense[t][:], planes[t][:].indirect(half_list(1)))
-            shared = HALF if t == EARLY[0] else HALF // 2
-            nc.scalar.copy(picked[1][:, :shared, t], dense[t][:, :shared])
-            if shared < HALF:
-                nc.gpsimd.tensor_copy(picked[1][:, shared:, t], dense[t][:, shared:])
-            nc.vector.tensor_copy(picked[0][:, :, t], planes[t][:].indirect(half_list(0)))
-        for a, b, who in CASTS:
-            if who == "scalar":
-                nc.scalar.copy(last_bf16[:, a:b], planes[PACK - 1][:, a:b])
+        for t in range(PACK - 1):
+            nc.vector.tensor_copy(picked[0][:, :, t], planes[t][:].indirect(entries(0, HALF)))
+            nc.scalar.activation(dense[t][:], planes[t][:].indirect(entries(HALF, S)), COPY)
+            nc.gpsimd.tensor_copy(picked[1][:, :BY_GPSIMD, t], dense[t][:, :BY_GPSIMD])
+            nc.scalar.copy(picked[1][:, BY_GPSIMD:, t], dense[t][:, BY_GPSIMD:])
+
+        last = PACK - 1
+        nc.vector.tensor_copy(picked[0][:, :, last], planes[last][:].indirect(entries(0, HALF)))
+        staged = {}
+        for a, b in LAST_GATHERS:
+            piece = keep.tile([P, b - a], BF16, name="staged%d" % a, tag="reused" if a == 0 else "staged%d" % a, align_bytes=64)
+            nc.scalar.activation(piece[:], planes[last][:].indirect(entries(HALF + a, HALF + b)), COPY)
+            staged[a] = (piece, b)
+        for a, b, who in LAST_PLACINGS:
+            start = max(s for s in staged if s <= a)
+            source = staged[start][0][:, a - start : b - start]
+            if who == "gpsimd":
+                nc.gpsimd.tensor_copy(picked[1][:, a:b, last], source)
             else:
-                nc.vector.tensor_copy(last_bf16[:, a:b], planes[PACK - 1][:, a:b])
-        nc.vector.tensor_copy(picked[0][:, :, PACK - 1], planes[PACK - 1][:].indirect(half_list(0)))
-        nc.scalar.activation(picked[1][:, :, PACK - 1], last_bf16[:].indirect(half_list(1)), COPY)
+                nc.scalar.copy(picked[1][:, a:b, last], source)
 
+        codes = [
+            keep.tile([P, HALF], U32, name="codes0", tag="reused", align_bytes=64),
+            keep.tile([P, HALF], U32, name="codes1", align_bytes=64),
+        ]
         for_vector = []
         for i, (a, b) in enumerate(PIECES):
             h, c = divmod(a, HALF)
-            codes = keep.tile([P, b - a], U32, name="codes%d" % i, align_bytes=64)
             scales = keep.tile([P, b - a], U8, name="scales%d" % i, align_bytes=64)
             nc.vector.quantize_mx(
-                out=codes[:].bitcast(FP8X4),
+                out=codes[h][:, c : c + b - a].bitcast(FP8X4),
                 scales=scales[:],
                 in_=picked[h][:, c : c + b - a, :].rearrange("p w t -> p (w t)"),
             )
@@ -95,12 +102,12 @@ def tile_picked_ranknet_tanh_e_kernel(tc, xT, w1_words, w1_scales, offs, win, lo
                 out=acc[:],
                 lhsT=w_codes[:].bitcast(FP8X4),
                 lhsT_scale=w_scales[:],
-                rhs=codes[:].bitcast(FP8X4),
+                rhs=codes[h][:, c : c + b - a].bitcast(FP8X4),
                 rhs_scale=scales[:],
                 start=True,
                 stop=True,
             )
-            if i in VECTOR_BANKS:
+            if i in VECTOR_PIECES:
                 for_vector.append((a, b, acc))
             else:
                 nc.scalar.copy(y[:, a:b], acc[:])
@@ -110,10 +117,15 @@ def tile_picked_ranknet_tanh_e_kernel(tc, xT, w1_words, w1_scales, offs, win, lo
         loser = keep.tile([P, V], F32, name="loser")
         diff = keep.tile([P, V], F32, name="diff")
         res = keep.tile([P, V], F32, name="res")
-        for a, b in LOSER_PIECES:
-            nc.vector.tensor_copy(loser[:, a:b], y[:].indirect(lose_sb[:, a // 16 : b // 16]))
+        for a, b, who in LOSERS:
+            source = y[:].indirect(lose_sb[:, a // 16 : b // 16])
+            if who == "scalar":
+                nc.scalar.activation(loser[:, a:b], source, COPY)
+            else:
+                nc.vector.tensor_copy(loser[:, a:b], source)
         for a, b in PAIR_PIECES:
-            nc.vector.tensor_tensor(diff[:, a:b], y[:].indirect(win_sb[:, a // 16 : b // 16]), loser[:, a:b], mybir.AluOpType.subtract)
+            nc.vector.tensor_tensor(diff[:, a:b], y[:].indirect(win_sb[:, a // 16 : b // 16]), loser[:, a:b], SUBTRACT)
+        for a, b in TANH_PIECES:
             nc.scalar.activation(res[:, a:b], diff[:, a:b], TANH)
         for a, b in STORES:
             (nc.scalar if b == V else nc.sync).dma_start(out[:, a:b], res[:, a:b])

@@ -19,16 +19,18 @@ SUBTRACT = mybir.AluOpType.subtract
 P = 128
 PACK = 4
 HALF = S // 2
+MULT = mybir.AluOpType.mult
+ADD = mybir.AluOpType.add
 BY_GPSIMD = 256
 LAST_GATHERS = ((0, 128), (128, 256), (256, 512))
 LAST_PLACINGS = ((0, 128, "gpsimd"), (128, 256, "gpsimd"), (256, 384, "scalar"), (384, 512, "scalar"))
 PIECES = ((512, 640), (0, 128), (128, 256), (256, 384), (384, 512), (640, 768), (768, 896), (896, 960), (960, 1024))
 BANKS = 8
 VECTOR_PIECES = (5, 7)
-LOSERS = ((0, 96, "vector"), (96, 192, "vector"), (192, 320, "scalar"), (320, 448, "scalar"), (448, 512, "scalar"))
-PAIR_PIECES = ((0, 96), (96, 192), (192, 320), (320, 448), (448, 512))
-TANH_PIECES = ((0, 192), (192, 320), (320, 448), (448, 512))
-STORES = ((0, 320), (320, 448), (448, 512))
+LOSERS = ((0, 64, "scalar"), (64, 224, "vector"), (224, 384, "scalar"), (384, 512, "scalar"))
+PAIR_PIECES = ((0, 64), (64, 224), (224, 384), (384, 448), (448, 512))
+TANH_PIECES = ((0, 224), (224, 384), (384, 448), (448, 512))
+STORES = ((0, 224), (224, 384), (384, 512))
 
 
 def tile_picked_ranknet_tanh_e_kernel(tc, xT, w1_words, w1_scales, offs, win, lose, out):
@@ -66,7 +68,7 @@ def tile_picked_ranknet_tanh_e_kernel(tc, xT, w1_words, w1_scales, offs, win, lo
         for t in range(PACK - 1):
             nc.vector.tensor_copy(picked[0][:, :, t], planes[t][:].indirect(entries(0, HALF)))
             nc.scalar.activation(dense[t][:], planes[t][:].indirect(entries(HALF, S)), COPY)
-            nc.gpsimd.tensor_copy(picked[1][:, :BY_GPSIMD, t], dense[t][:, :BY_GPSIMD])
+            nc.gpsimd.tensor_scalar(picked[1][:, :BY_GPSIMD, t], dense[t][:, :BY_GPSIMD], 1.0, 0.0, MULT, ADD)
             nc.scalar.copy(picked[1][:, BY_GPSIMD:, t], dense[t][:, BY_GPSIMD:])
 
         last = PACK - 1
@@ -80,7 +82,7 @@ def tile_picked_ranknet_tanh_e_kernel(tc, xT, w1_words, w1_scales, offs, win, lo
             start = max(s for s in staged if s <= a)
             source = staged[start][0][:, a - start : b - start]
             if who == "gpsimd":
-                nc.gpsimd.tensor_copy(picked[1][:, a:b, last], source)
+                nc.gpsimd.tensor_scalar(picked[1][:, a:b, last], source, 1.0, 0.0, MULT, ADD)
             else:
                 nc.scalar.copy(picked[1][:, a:b, last], source)
 

@@ -18,19 +18,19 @@ SUBTRACT = mybir.AluOpType.subtract
 
 P = 128
 PACK = 4
-HALF = S // 2
 MULT = mybir.AluOpType.mult
 ADD = mybir.AluOpType.add
-BY_GPSIMD = 256
-LAST_GATHERS = ((0, 128), (128, 256), (256, 512))
-LAST_PLACINGS = ((0, 128, "gpsimd"), (128, 256, "gpsimd"), (256, 384, "scalar"), (384, 512, "scalar"))
-PIECES = ((512, 640), (0, 128), (128, 256), (256, 384), (384, 512), (640, 768), (768, 896), (896, 960), (960, 1024))
+BY_VECTOR = (256, 800)
+EARLY_GATHERS = ((0, 256), (800, 1024))
+LAST_GATHERS = ((0, 128), (128, 256), (800, 896), (896, 1024))
+LAST_PLACINGS = ((0, 128), (128, 256), (800, 896), (896, 960), (960, 1024))
+PIECES = ((0, 128), (128, 256), (256, 384), (384, 512), (512, 640), (640, 768), (768, 896), (896, 960), (960, 1024))
 BANKS = 8
 VECTOR_PIECES = (5, 7)
-LOSERS = ((0, 64, "scalar"), (64, 224, "vector"), (224, 384, "scalar"), (384, 512, "scalar"))
-PAIR_PIECES = ((0, 64), (64, 224), (224, 384), (384, 448), (448, 512))
-TANH_PIECES = ((0, 224), (224, 384), (384, 448), (448, 512))
-STORES = ((0, 224), (224, 384), (384, 512))
+LOSERS = ((0, 96, "vector"), (96, 192, "vector"), (192, 320, "scalar"), (320, 448, "scalar"), (448, 512, "scalar"))
+PAIR_PIECES = ((0, 96), (96, 192), (192, 320), (320, 448), (448, 512))
+TANH_PIECES = ((0, 192), (192, 320), (320, 448), (448, 512))
+STORES = ((0, 320), (320, 448), (448, 512))
 
 
 def tile_picked_ranknet_tanh_e_kernel(tc, xT, w1_words, w1_scales, offs, win, lose, out):
@@ -43,8 +43,7 @@ def tile_picked_ranknet_tanh_e_kernel(tc, xT, w1_words, w1_scales, offs, win, lo
         win_sb = keep.tile([P, V // 16], U16, name="win_sb")
         lose_sb = keep.tile([P, V // 16], U16, name="lose_sb")
         planes = [keep.tile([P, T], F32, name="plane%d" % t, align_bytes=64) for t in range(PACK)]
-        picked = [keep.tile([P, HALF, PACK], BF16, name="picked%d" % h, align_bytes=64) for h in range(2)]
-        dense = [keep.tile([P, HALF], BF16, name="dense%d" % t, align_bytes=64) for t in range(PACK - 1)]
+        picked = keep.tile([P, S, PACK], BF16, name="picked", align_bytes=64)
         w_codes = keep.tile([P, N], U32, name="w_codes", align_bytes=64)
         w_scales = keep.tile([P, N], U8, name="w_scales", align_bytes=64)
         y = keep.tile([P, S], F32, name="y", align_bytes=64)
@@ -62,49 +61,42 @@ def tile_picked_ranknet_tanh_e_kernel(tc, xT, w1_words, w1_scales, offs, win, lo
         nc.sync.dma_start(lose_sb[:], lose)
         nc.sync.dma_start(win_sb[:], win)
 
-        def entries(a, b):
-            return offs_sb[:, a // 16 : b // 16]
+        def looked_up(t, a, b):
+            return planes[t][:].indirect(offs_sb[:, a // 16 : b // 16])
 
-        for t in range(PACK - 1):
-            nc.vector.tensor_copy(picked[0][:, :, t], planes[t][:].indirect(entries(0, HALF)))
-            nc.scalar.activation(dense[t][:], planes[t][:].indirect(entries(HALF, S)), COPY)
-            nc.gpsimd.tensor_scalar(picked[1][:, :BY_GPSIMD, t], dense[t][:, :BY_GPSIMD], 1.0, 0.0, MULT, ADD)
-            nc.scalar.copy(picked[1][:, BY_GPSIMD:, t], dense[t][:, BY_GPSIMD:])
+        for t in range(PACK):
+            last = t == PACK - 1
+            nc.vector.tensor_copy(picked[:, BY_VECTOR[0] : BY_VECTOR[1], t], looked_up(t, *BY_VECTOR))
+            staged = []
+            for a, b in LAST_GATHERS if last else EARLY_GATHERS:
+                name = "staged%d_%d" % (t, a)
+                piece = keep.tile([P, b - a], F32, name=name, tag="reused" if last and a == 0 else name, align_bytes=64)
+                nc.scalar.activation(piece[:], looked_up(t, a, b), COPY)
+                staged.append((a, b, piece))
+            for a, b in LAST_PLACINGS if last else EARLY_GATHERS:
+                start, piece = [(c, piece) for c, d, piece in staged if c <= a < d][0]
+                if b <= BY_VECTOR[0]:
+                    nc.gpsimd.tensor_scalar(picked[:, a:b, t], piece[:, a - start : b - start], 1.0, 0.0, MULT, ADD)
+                else:
+                    nc.scalar.copy(picked[:, a:b, t], piece[:, a - start : b - start])
 
-        last = PACK - 1
-        nc.vector.tensor_copy(picked[0][:, :, last], planes[last][:].indirect(entries(0, HALF)))
-        staged = {}
-        for a, b in LAST_GATHERS:
-            piece = keep.tile([P, b - a], BF16, name="staged%d" % a, tag="reused" if a == 0 else "staged%d" % a, align_bytes=64)
-            nc.scalar.activation(piece[:], planes[last][:].indirect(entries(HALF + a, HALF + b)), COPY)
-            staged[a] = (piece, b)
-        for a, b, who in LAST_PLACINGS:
-            start = max(s for s in staged if s <= a)
-            source = staged[start][0][:, a - start : b - start]
-            if who == "gpsimd":
-                nc.gpsimd.tensor_scalar(picked[1][:, a:b, last], source, 1.0, 0.0, MULT, ADD)
-            else:
-                nc.scalar.copy(picked[1][:, a:b, last], source)
-
-        codes = [
-            keep.tile([P, HALF], U32, name="codes0", tag="reused", align_bytes=64),
-            keep.tile([P, HALF], U32, name="codes1", align_bytes=64),
-        ]
+        first_codes = keep.tile([P, BY_VECTOR[0]], U32, name="first_codes", align_bytes=64)
+        later_codes = keep.tile([P, S - BY_VECTOR[0]], U32, name="later_codes", tag="reused", align_bytes=64)
         for_vector = []
         for i, (a, b) in enumerate(PIECES):
-            h, c = divmod(a, HALF)
+            codes = first_codes[:, a:b] if b <= BY_VECTOR[0] else later_codes[:, a - BY_VECTOR[0] : b - BY_VECTOR[0]]
             scales = keep.tile([P, b - a], U8, name="scales%d" % i, align_bytes=64)
             nc.vector.quantize_mx(
-                out=codes[h][:, c : c + b - a].bitcast(FP8X4),
+                out=codes.bitcast(FP8X4),
                 scales=scales[:],
-                in_=picked[h][:, c : c + b - a, :].rearrange("p w t -> p (w t)"),
+                in_=picked[:, a:b, :].rearrange("p w t -> p (w t)"),
             )
             acc = psum.tile([P, b - a], F32, name="acc%d" % (i % BANKS))
             nc.tensor.matmul_mx(
                 out=acc[:],
                 lhsT=w_codes[:].bitcast(FP8X4),
                 lhsT_scale=w_scales[:],
-                rhs=codes[h][:, c : c + b - a].bitcast(FP8X4),
+                rhs=codes.bitcast(FP8X4),
                 rhs_scale=scales[:],
                 start=True,
                 stop=True,

@@ -20,10 +20,10 @@ P = 128
 PACK = 4
 MULT = mybir.AluOpType.mult
 ADD = mybir.AluOpType.add
-BY_VECTOR = (256, 800)
-EARLY_GATHERS = ((0, 256), (800, 1024))
-LAST_GATHERS = ((0, 128), (128, 256), (800, 896), (896, 1024))
-LAST_PLACINGS = ((0, 128), (128, 256), (800, 896), (896, 960), (960, 1024))
+BY_VECTOR = (256, 768)
+EARLY_GATHERS = ((0, 256), (768, 1024))
+LAST_GATHERS = ((0, 128), (128, 256), (768, 896), (896, 1024))
+LAST_PLACINGS = ((0, 128), (128, 256), (768, 896), (896, 960), (960, 1024))
 PIECES = ((0, 128), (128, 256), (256, 384), (384, 512), (512, 640), (640, 768), (768, 896), (896, 960), (960, 1024))
 BANKS = 8
 VECTOR_PIECES = (5, 7)

@@ -30,7 +30,7 @@ VECTOR_PIECES = (5, 7)
 LOSERS = ((0, 96, "vector"), (96, 192, "vector"), (192, 320, "scalar"), (320, 448, "scalar"), (448, 512, "scalar"))
 PAIR_PIECES = ((0, 96), (96, 192), (192, 320), (320, 448), (448, 512))
 TANH_PIECES = ((0, 192), (192, 320), (320, 448), (448, 512))
-STORES = ((0, 320), (320, 448), (448, 512))
+STORES = ((0, 320), (320, 512))
 
 
 def tile_picked_ranknet_tanh_e_kernel(tc, xT, w1_words, w1_scales, offs, win, lose, out):
@@ -55,7 +55,9 @@ def tile_picked_ranknet_tanh_e_kernel(tc, xT, w1_words, w1_scales, offs, win, lo
         nc.sync.dma_start(offs_sb[:], offs)
         for t in range(1, PACK):
             nc.sync.dma_start(planes[t][:], rows[:, t, :])
-        nc.sync.dma_start(w_codes[:].bitcast(I32), w1_words[0].rearrange("p n t -> p (n t)").bitcast(I32))
+        w_words = w1_words[0].rearrange("p n t -> p (n t)").bitcast(I32)
+        for a in range(0, N, N // 2):
+            nc.sync.dma_start(w_codes[:, a : a + N // 2].bitcast(I32), w_words[:, a : a + N // 2])
         for q in range(4):
             nc.sync.dma_start(w_scales[32 * q : 32 * q + 4, :].bitcast(I32), w1_scales[0, 4 * q : 4 * q + 4, :].bitcast(I32))
         nc.sync.dma_start(lose_sb[:], lose)

@@ -27,10 +27,11 @@ LAST_PLACINGS = ((0, 128), (128, 256), (768, 896), (896, 960), (960, 1024))
 PIECES = ((0, 128), (128, 256), (256, 384), (384, 512), (512, 640), (640, 768), (768, 896), (896, 960), (960, 1024))
 BANKS = 8
 VECTOR_PIECES = (5, 7)
-LOSERS = ((0, 96, "vector"), (96, 192, "vector"), (192, 320, "scalar"), (320, 448, "scalar"), (448, 512, "scalar"))
-PAIR_PIECES = ((0, 96), (96, 192), (192, 320), (320, 448), (448, 512))
-TANH_PIECES = ((0, 192), (192, 320), (320, 448), (448, 512))
-STORES = ((0, 320), (320, 512))
+LOSERS = ((64, 256, "vector"), (0, 64, "scalar"), (256, 384, "scalar"), (384, 512, "scalar"))
+PAIR_PIECES = ((0, 64), (64, 256), (256, 384), (384, 448))
+BOTH_BY_SCALAR = (448, 512)
+TANH_PIECES = ((0, 256), (256, 384), (384, 448), (448, 512))
+STORES = ((0, 256), (256, 384), (384, 512))
 
 
 def tile_picked_ranknet_tanh_e_kernel(tc, xT, w1_words, w1_scales, offs, win, lose, out):
@@ -121,7 +122,11 @@ def tile_picked_ranknet_tanh_e_kernel(tc, xT, w1_words, w1_scales, offs, win, lo
                 nc.vector.tensor_copy(loser[:, a:b], source)
         for a, b in PAIR_PIECES:
             nc.vector.tensor_tensor(diff[:, a:b], y[:].indirect(win_sb[:, a // 16 : b // 16]), loser[:, a:b], SUBTRACT)
+        a, b = BOTH_BY_SCALAR
+        winner = keep.tile([P, b - a], F32, name="winner")
+        nc.scalar.activation(winner[:], y[:].indirect(win_sb[:, a // 16 : b // 16]), COPY)
+        nc.vector.tensor_tensor(diff[:, a:b], winner[:], loser[:, a:b], SUBTRACT)
         for a, b in TANH_PIECES:
             nc.scalar.activation(res[:, a:b], diff[:, a:b], TANH)
         for a, b in STORES:
-            (nc.scalar if b == V else nc.sync).dma_start(out[:, a:b], res[:, a:b])
+            nc.sync.dma_start(out[:, a:b], res[:, a:b])

@@ -25,8 +25,9 @@ EARLY_GATHERS = ((0, 256), (768, 1024))
 LAST_GATHERS = ((0, 128), (128, 256), (768, 896), (896, 1024))
 LAST_PLACINGS = ((0, 128), (128, 256), (768, 896), (896, 960), (960, 1024))
 PIECES = ((0, 128), (128, 256), (256, 384), (384, 512), (512, 640), (640, 768), (768, 896), (896, 960), (960, 1024))
+WEIGHT_LOADS = ((0, 64), (64, 96), (96, 128))
 BANKS = 8
-VECTOR_PIECES = (5, 7)
+VECTOR_PIECES = (3, 5, 7)
 LOSERS = ((64, 256, "vector"), (0, 64, "scalar"), (256, 384, "scalar"), (384, 512, "scalar"))
 PAIR_PIECES = ((0, 64), (64, 256), (256, 384), (384, 448))
 BOTH_BY_SCALAR = (448, 512)
@@ -43,7 +44,9 @@ def tile_picked_ranknet_tanh_e_kernel(tc, xT, w1_words, w1_scales, offs, win, lo
         offs_sb = keep.tile([P, S // 16], U16, name="offs_sb")
         win_sb = keep.tile([P, V // 16], U16, name="win_sb")
         lose_sb = keep.tile([P, V // 16], U16, name="lose_sb")
-        planes = [keep.tile([P, T], F32, name="plane%d" % t, align_bytes=64) for t in range(PACK)]
+        first_two = keep.tile([P, 2, T], F32, name="first_two", align_bytes=64)
+        planes = [first_two[:, 0, :], first_two[:, 1, :]]
+        planes = planes + [keep.tile([P, T], F32, name="plane%d" % t, align_bytes=64)[:] for t in range(2, PACK)]
         picked = keep.tile([P, S, PACK], BF16, name="picked", align_bytes=64)
         w_codes = keep.tile([P, N], U32, name="w_codes", align_bytes=64)
         w_scales = keep.tile([P, N], U8, name="w_scales", align_bytes=64)
@@ -52,20 +55,20 @@ def tile_picked_ranknet_tanh_e_kernel(tc, xT, w1_words, w1_scales, offs, win, lo
         nc.vector.memset(w_scales[:].bitcast(I32), 0)
 
         rows = xT.rearrange("(p t) w -> p t w", t=PACK)
-        nc.sync.dma_start(planes[0][:], rows[:, 0, :])
+        nc.sync.dma_start(first_two[:], rows[:, 0:2, :])
         nc.sync.dma_start(offs_sb[:], offs)
-        for t in range(1, PACK):
-            nc.sync.dma_start(planes[t][:], rows[:, t, :])
+        for t in range(2, PACK):
+            nc.sync.dma_start(planes[t], rows[:, t, :])
         w_words = w1_words[0].rearrange("p n t -> p (n t)").bitcast(I32)
-        for a in range(0, N, N // 2):
-            nc.sync.dma_start(w_codes[:, a : a + N // 2].bitcast(I32), w_words[:, a : a + N // 2])
+        for a, b in WEIGHT_LOADS:
+            nc.sync.dma_start(w_codes[:, a:b].bitcast(I32), w_words[:, a:b])
         for q in range(4):
             nc.sync.dma_start(w_scales[32 * q : 32 * q + 4, :].bitcast(I32), w1_scales[0, 4 * q : 4 * q + 4, :].bitcast(I32))
         nc.sync.dma_start(lose_sb[:], lose)
         nc.sync.dma_start(win_sb[:], win)
 
         def looked_up(t, a, b):
-            return planes[t][:].indirect(offs_sb[:, a // 16 : b // 16])
+            return planes[t].indirect(offs_sb[:, a // 16 : b // 16])
 
         for t in range(PACK):
             last = t == PACK - 1
@@ -78,7 +81,7 @@ def tile_picked_ranknet_tanh_e_kernel(tc, xT, w1_words, w1_scales, offs, win, lo
                 staged.append((a, b, piece))
             for a, b in LAST_PLACINGS if last else EARLY_GATHERS:
                 start, piece = [(c, piece) for c, d, piece in staged if c <= a < d][0]
-                if b <= BY_VECTOR[0]:
+                if b <= BY_VECTOR[0] or t < 2:
                     nc.gpsimd.tensor_scalar(picked[:, a:b, t], piece[:, a - start : b - start], 1.0, 0.0, MULT, ADD)
                 else:
                     nc.scalar.copy(picked[:, a:b, t], piece[:, a - start : b - start])

@@ -28,11 +28,11 @@ PIECES = ((0, 128), (128, 256), (256, 384), (384, 512), (512, 640), (640, 768), 
 WEIGHT_LOADS = ((0, 64), (64, 96), (96, 128))
 BANKS = 8
 VECTOR_PIECES = (3, 5, 7)
-LOSERS = ((64, 256, "vector"), (0, 64, "scalar"), (256, 384, "scalar"), (384, 512, "scalar"))
-PAIR_PIECES = ((0, 64), (64, 256), (256, 384), (384, 448))
+LOSERS = ((64, 224, "vector"), (0, 64, "scalar"), (224, 384, "scalar"), (384, 512, "scalar"))
+PAIR_PIECES = ((0, 64), (64, 224), (224, 384), (384, 448))
 BOTH_BY_SCALAR = (448, 512)
-TANH_PIECES = ((0, 256), (256, 384), (384, 448), (448, 512))
-STORES = ((0, 256), (256, 384), (384, 512))
+TANH_PIECES = ((0, 224), (224, 384), (384, 448), (448, 512))
+STORES = ((0, 224), (224, 384), (384, 512))
 
 
 def tile_picked_ranknet_tanh_e_kernel(tc, xT, w1_words, w1_scales, offs, win, lose, out):

@@ -25,7 +25,7 @@ EARLY_GATHERS = ((0, 256), (768, 1024))
 LAST_GATHERS = ((0, 128), (128, 256), (768, 896), (896, 1024))
 LAST_PLACINGS = ((0, 128), (128, 256), (768, 896), (896, 960), (960, 1024))
 PIECES = ((0, 128), (128, 256), (256, 384), (384, 512), (512, 640), (640, 768), (768, 896), (896, 960), (960, 1024))
-WEIGHT_LOADS = ((0, 64), (64, 96), (96, 128))
+SCALE_LOADS = ((0, 4), (4, 8), (8, 12), (12, 14), (14, 16))
 BANKS = 8
 VECTOR_PIECES = (3, 5, 7)
 LOSERS = ((64, 224, "vector"), (0, 64, "scalar"), (224, 384, "scalar"), (384, 512, "scalar"))
@@ -44,9 +44,10 @@ def tile_picked_ranknet_tanh_e_kernel(tc, xT, w1_words, w1_scales, offs, win, lo
         offs_sb = keep.tile([P, S // 16], U16, name="offs_sb")
         win_sb = keep.tile([P, V // 16], U16, name="win_sb")
         lose_sb = keep.tile([P, V // 16], U16, name="lose_sb")
-        first_two = keep.tile([P, 2, T], F32, name="first_two", align_bytes=64)
-        planes = [first_two[:, 0, :], first_two[:, 1, :]]
-        planes = planes + [keep.tile([P, T], F32, name="plane%d" % t, align_bytes=64)[:] for t in range(2, PACK)]
+        first = keep.tile([P, T], F32, name="first", align_bytes=64)
+        middle = keep.tile([P, 2, T], F32, name="middle", align_bytes=64)
+        final = keep.tile([P, T], F32, name="final", align_bytes=64)
+        planes = [middle[:, 0, :], middle[:, 1, :], first[:], final[:]]
         picked = keep.tile([P, S, PACK], BF16, name="picked", align_bytes=64)
         w_codes = keep.tile([P, N], U32, name="w_codes", align_bytes=64)
         w_scales = keep.tile([P, N], U8, name="w_scales", align_bytes=64)
@@ -55,22 +56,23 @@ def tile_picked_ranknet_tanh_e_kernel(tc, xT, w1_words, w1_scales, offs, win, lo
         nc.vector.memset(w_scales[:].bitcast(I32), 0)
 
         rows = xT.rearrange("(p t) w -> p t w", t=PACK)
-        nc.sync.dma_start(first_two[:], rows[:, 0:2, :])
-        nc.sync.dma_start(offs_sb[:], offs)
-        for t in range(2, PACK):
-            nc.sync.dma_start(planes[t], rows[:, t, :])
         w_words = w1_words[0].rearrange("p n t -> p (n t)").bitcast(I32)
-        for a, b in WEIGHT_LOADS:
+        nc.sync.dma_start(offs_sb[:], offs)
+        nc.scalar.dma_start(first[:], rows[:, 2, :])
+        nc.sync.dma_start(middle[:], rows[:, 0:2, :])
+        nc.sync.dma_start(final[:], rows[:, 3, :])
+        for a, b in ((0, N // 2), (N // 2, N)):
             nc.sync.dma_start(w_codes[:, a:b].bitcast(I32), w_words[:, a:b])
-        for q in range(4):
-            nc.sync.dma_start(w_scales[32 * q : 32 * q + 4, :].bitcast(I32), w1_scales[0, 4 * q : 4 * q + 4, :].bitcast(I32))
+        for a, b in SCALE_LOADS:
+            first_row = 32 * (a // 4) + a % 4
+            nc.sync.dma_start(w_scales[first_row : first_row + b - a, :].bitcast(I32), w1_scales[0, a:b, :].bitcast(I32))
         nc.sync.dma_start(lose_sb[:], lose)
         nc.sync.dma_start(win_sb[:], win)
 
         def looked_up(t, a, b):
             return planes[t].indirect(offs_sb[:, a // 16 : b // 16])
 
-        for t in range(PACK):
+        for t in (2, 0, 1, 3):
             last = t == PACK - 1
             nc.vector.tensor_copy(picked[:, BY_VECTOR[0] : BY_VECTOR[1], t], looked_up(t, *BY_VECTOR))
             staged = []

@@ -77,13 +77,19 @@ def tile_picked_ranknet_tanh_e_kernel(tc, xT, w1_words, w1_scales, offs, win, lo
             nc.vector.tensor_copy(picked[:, BY_VECTOR[0] : BY_VECTOR[1], t], looked_up(t, *BY_VECTOR))
             staged = []
             for a, b in LAST_GATHERS if last else EARLY_GATHERS:
-                name = "staged%d_%d" % (t, a)
-                piece = keep.tile([P, b - a], F32, name=name, tag="reused" if last and a == 0 else name, align_bytes=64)
-                nc.scalar.activation(piece[:], looked_up(t, a, b), COPY)
+                if last and a >= BY_VECTOR[1]:
+                    piece = partner[:, a - BY_VECTOR[1] : b - BY_VECTOR[1]]
+                else:
+                    name = "staged%d_%d" % (t, a)
+                    tag = "reused" if last and a == 0 else name
+                    piece = keep.tile([P, b - a], F32, name=name, tag=tag, align_bytes=64)[:]
+                if t == PACK - 2 and a >= BY_VECTOR[1]:
+                    partner = piece
+                nc.scalar.activation(piece, looked_up(t, a, b), COPY)
                 staged.append((a, b, piece))
             for a, b in LAST_PLACINGS if last else EARLY_GATHERS:
                 start, piece = [(c, piece) for c, d, piece in staged if c <= a < d][0]
-                if b <= BY_VECTOR[0] or t < 2:
+                if b <= BY_VECTOR[0] or not last:
                     nc.gpsimd.tensor_scalar(picked[:, a:b, t], piece[:, a - start : b - start], 1.0, 0.0, MULT, ADD)
                 else:
                     nc.scalar.copy(picked[:, a:b, t], piece[:, a - start : b - start])

@@ -22,8 +22,8 @@ MULT = mybir.AluOpType.mult
 ADD = mybir.AluOpType.add
 BY_VECTOR = (256, 768)
 EARLY_GATHERS = ((0, 256), (768, 1024))
-LAST_GATHERS = ((0, 128), (128, 256), (768, 896), (896, 1024))
-LAST_PLACINGS = ((0, 128), (128, 256), (768, 896), (896, 960), (960, 1024))
+LAST_GATHERS = ((0, 64), (64, 160), (160, 256), (768, 896), (896, 1024))
+LAST_PLACINGS = ((0, 64), (64, 160), (160, 256), (768, 896), (896, 960), (960, 1024))
 PIECES = ((0, 128), (128, 256), (256, 384), (384, 512), (512, 640), (640, 768), (768, 896), (896, 960), (960, 1024))
 SCALE_LOADS = ((0, 4), (4, 8), (8, 12), (12, 14), (14, 16))
 BANKS = 8
@@ -81,7 +81,7 @@ def tile_picked_ranknet_tanh_e_kernel(tc, xT, w1_words, w1_scales, offs, win, lo
                     piece = partner[:, a - BY_VECTOR[1] : b - BY_VECTOR[1]]
                 else:
                     name = "staged%d_%d" % (t, a)
-                    tag = "reused" if last and a == 0 else name
+                    tag = "reused" if last and b == BY_VECTOR[0] else name
                     piece = keep.tile([P, b - a], F32, name=name, tag=tag, align_bytes=64)[:]
                 if t == PACK - 2 and a >= BY_VECTOR[1]:
                     partner = piece

from contextlib import ExitStack

import concourse.mybir as mybir

K, T, S, V, N = 512, 4096, 1024, 512, 128
FLOPS = 2 * K * S * N

F32 = mybir.dt.float32
BF16 = mybir.dt.bfloat16
I32 = mybir.dt.int32
U32 = mybir.dt.uint32
U16 = mybir.dt.uint16
U8 = mybir.dt.uint8
FP8X4 = mybir.dt.float8_e4m3fn_x4
COPY = mybir.ActivationFunctionType.Copy
TANH = mybir.ActivationFunctionType.Tanh
SUBTRACT = mybir.AluOpType.subtract

P = 128
PACK = 4
MULT = mybir.AluOpType.mult
ADD = mybir.AluOpType.add
BY_VECTOR = (256, 768)
EARLY_GATHERS = ((0, 256), (768, 1024))
LAST_GATHERS = ((0, 64), (64, 160), (160, 256), (768, 896), (896, 1024))
LAST_PLACINGS = ((0, 64), (64, 160), (160, 256), (768, 896), (896, 960), (960, 1024))
PIECES = ((0, 128), (128, 256), (256, 384), (384, 512), (512, 640), (640, 768), (768, 896), (896, 960), (960, 1024))
SCALE_LOADS = ((0, 4), (4, 8), (8, 12), (12, 14), (14, 16))
BANKS = 8
VECTOR_PIECES = (3, 5, 7)
LOSERS = ((64, 224, "vector"), (0, 64, "scalar"), (224, 384, "scalar"), (384, 512, "scalar"))
PAIR_PIECES = ((0, 64), (64, 224), (224, 384), (384, 448))
BOTH_BY_SCALAR = (448, 512)
TANH_PIECES = ((0, 224), (224, 384), (384, 448), (448, 512))
STORES = ((0, 224), (224, 384), (384, 512))


def tile_picked_ranknet_tanh_e_kernel(tc, xT, w1_words, w1_scales, offs, win, lose, out):
    nc = tc.nc
    with ExitStack() as ctx:
        keep = ctx.enter_context(tc.tile_pool(name="keep", bufs=1))
        psum = ctx.enter_context(tc.psum_pool(name="psum", bufs=1))

        offs_sb = keep.tile([P, S // 16], U16, name="offs_sb")
        win_sb = keep.tile([P, V // 16], U16, name="win_sb")
        lose_sb = keep.tile([P, V // 16], U16, name="lose_sb")
        first = keep.tile([P, T], F32, name="first", align_bytes=64)
        middle = keep.tile([P, 2, T], F32, name="middle", align_bytes=64)
        final = keep.tile([P, T], F32, name="final", align_bytes=64)
        planes = [middle[:, 0, :], middle[:, 1, :], first[:], final[:]]
        picked = keep.tile([P, S, PACK], BF16, name="picked", align_bytes=64)
        w_codes = keep.tile([P, N], U32, name="w_codes", align_bytes=64)
        w_scales = keep.tile([P, N], U8, name="w_scales", align_bytes=64)
        y = keep.tile([P, S], F32, name="y", align_bytes=64)

        nc.vector.memset(w_scales[:].bitcast(I32), 0)

        rows = xT.rearrange("(p t) w -> p t w", t=PACK)
        w_words = w1_words[0].rearrange("p n t -> p (n t)").bitcast(I32)
        nc.sync.dma_start(offs_sb[:], offs)
        nc.scalar.dma_start(first[:], rows[:, 2, :])
        nc.sync.dma_start(middle[:], rows[:, 0:2, :])
        nc.sync.dma_start(final[:], rows[:, 3, :])
        for a, b in ((0, N // 2), (N // 2, N)):
            nc.sync.dma_start(w_codes[:, a:b].bitcast(I32), w_words[:, a:b])
        for a, b in SCALE_LOADS:
            first_row = 32 * (a // 4) + a % 4
            nc.sync.dma_start(w_scales[first_row : first_row + b - a, :].bitcast(I32), w1_scales[0, a:b, :].bitcast(I32))
        nc.sync.dma_start(lose_sb[:], lose)
        nc.sync.dma_start(win_sb[:], win)

        def looked_up(t, a, b):
            return planes[t].indirect(offs_sb[:, a // 16 : b // 16])

        for t in (2, 0, 1, 3):
            last = t == PACK - 1
            nc.vector.tensor_copy(picked[:, BY_VECTOR[0] : BY_VECTOR[1], t], looked_up(t, *BY_VECTOR))
            staged = []
            for a, b in LAST_GATHERS if last else EARLY_GATHERS:
                if last and a >= BY_VECTOR[1]:
                    piece = partner[:, a - BY_VECTOR[1] : b - BY_VECTOR[1]]
                else:
                    name = "staged%d_%d" % (t, a)
                    tag = "reused" if last and b == BY_VECTOR[0] else name
                    piece = keep.tile([P, b - a], F32, name=name, tag=tag, align_bytes=64)[:]
                if t == PACK - 2 and a >= BY_VECTOR[1]:
                    partner = piece
                nc.scalar.activation(piece, looked_up(t, a, b), COPY)
                staged.append((a, b, piece))
            for a, b in LAST_PLACINGS if last else EARLY_GATHERS:
                start, piece = [(c, piece) for c, d, piece in staged if c <= a < d][0]
                if b <= BY_VECTOR[0] or not last:
                    nc.gpsimd.tensor_scalar(picked[:, a:b, t], piece[:, a - start : b - start], 1.0, 0.0, MULT, ADD)
                else:
                    nc.scalar.copy(picked[:, a:b, t], piece[:, a - start : b - start])

        first_codes = keep.tile([P, BY_VECTOR[0]], U32, name="first_codes", align_bytes=64)
        later_codes = keep.tile([P, S - BY_VECTOR[0]], U32, name="later_codes", tag="reused", align_bytes=64)
        for_vector = []
        for i, (a, b) in enumerate(PIECES):
            codes = first_codes[:, a:b] if b <= BY_VECTOR[0] else later_codes[:, a - BY_VECTOR[0] : b - BY_VECTOR[0]]
            scales = keep.tile([P, b - a], U8, name="scales%d" % i, align_bytes=64)
            nc.vector.quantize_mx(
                out=codes.bitcast(FP8X4),
                scales=scales[:],
                in_=picked[:, a:b, :].rearrange("p w t -> p (w t)"),
            )
            acc = psum.tile([P, b - a], F32, name="acc%d" % (i % BANKS))
            nc.tensor.matmul_mx(
                out=acc[:],
                lhsT=w_codes[:].bitcast(FP8X4),
                lhsT_scale=w_scales[:],
                rhs=codes.bitcast(FP8X4),
                rhs_scale=scales[:],
                start=True,
                stop=True,
            )
            if i in VECTOR_PIECES:
                for_vector.append((a, b, acc))
            else:
                nc.scalar.copy(y[:, a:b], acc[:])
        for a, b, acc in for_vector:
            nc.vector.tensor_copy(y[:, a:b], acc[:])

        loser = keep.tile([P, V], F32, name="loser")
        diff = keep.tile([P, V], F32, name="diff")
        res = keep.tile([P, V], F32, name="res")
        for a, b, who in LOSERS:
            source = y[:].indirect(lose_sb[:, a // 16 : b // 16])
            if who == "scalar":
                nc.scalar.activation(loser[:, a:b], source, COPY)
            else:
                nc.vector.tensor_copy(loser[:, a:b], source)
        for a, b in PAIR_PIECES:
            nc.vector.tensor_tensor(diff[:, a:b], y[:].indirect(win_sb[:, a // 16 : b // 16]), loser[:, a:b], SUBTRACT)
        a, b = BOTH_BY_SCALAR
        winner = keep.tile([P, b - a], F32, name="winner")
        nc.scalar.activation(winner[:], y[:].indirect(win_sb[:, a // 16 : b // 16]), COPY)
        nc.vector.tensor_tensor(diff[:, a:b], winner[:], loser[:, a:b], SUBTRACT)
        for a, b in TANH_PIECES:
            nc.scalar.activation(res[:, a:b], diff[:, a:b], TANH)
        for a, b in STORES:
            nc.sync.dma_start(out[:, a:b], res[:, a:b])
